import numpy as np
import ml_dtypes


def mxq(x, axis, fmt="e4m3"):
    dtype, down = {"e4m3": (ml_dtypes.float8_e4m3fn, 7), "e5m2": (ml_dtypes.float8_e5m2, 14)}[fmt]
    v = np.moveaxis(np.asarray(x, np.float32).astype(ml_dtypes.bfloat16).astype(np.float64), axis, -1)
    blocks = v.reshape(v.shape[:-1] + (-1, 32))
    amax = np.abs(blocks).max(-1, keepdims=True)
    byte = np.maximum(np.where(amax > 0, np.frexp(amax)[1] - 1 + 127, 0) - down, 1)
    scale = np.exp2(byte - 127.0)
    codes = (blocks / scale).astype(np.float32).astype(dtype).astype(np.float64)
    return np.moveaxis((codes * scale).reshape(v.shape), -1, axis)


WIDE = False


def mx_kscale(k):
    if not WIDE:
        return np.ones(k)
    levels = np.array([10, -10, 5, -5, 0])
    if k % 512:
        return np.exp2(np.random.permutation(np.resize(levels, k // 32))).repeat(32)
    a = np.empty((k // 512, 16))
    for p in range(k // 512):
        a[p, :8] = np.random.permutation(np.resize(levels, 8))
        for g in range(8):
            far = levels[np.abs(levels - a[p, g]) >= 10]
            a[p, g + 8] = far[np.random.randint(len(far))]
    return np.exp2(a.ravel()).repeat(32)


def f64(x):
    return np.asarray(x).astype(np.float64)


def striped(idx):
    return np.tile(idx.reshape(-1, 16).T, (8, 1)).astype(np.uint16)


def unstriped(offs):
    return offs[:16].T.reshape(-1).astype(np.int64)


E2M1 = np.array([0.0, 0.5, 1.0, 1.5, 2.0, 3.0, 4.0, 6.0, -0.0, -0.5, -1.0, -1.5, -2.0, -3.0, -4.0, -6.0])


def pack_weight(w, fmt):
    k, n = w.shape
    w = f64(np.asarray(w, np.float32).astype(ml_dtypes.bfloat16)).reshape(k // 32, 32, n)
    amax = np.abs(w).max(1)
    if fmt == "e4m3":
        byte = np.frexp(amax)[1] - 1 + 127 - 7
    else:
        mant, ex = np.frexp(amax / 6.0)
        byte = np.where(mant > 0.5, ex, ex - 1) + 127
    byte = np.clip(np.where(amax > 0, byte, 1), 1, 254)
    scaled = (w * np.exp2(127.0 - byte)[:, None, :]).reshape(k, n).astype(np.float32)
    by_word = np.ascontiguousarray(scaled.reshape(k // 512, 128, 4, n).transpose(0, 1, 3, 2))
    if fmt == "e4m3":
        words = by_word.astype(ml_dtypes.float8_e4m3fn).view(np.uint8)
    else:
        c = by_word.astype(ml_dtypes.float4_e2m1fn).view(np.uint8) & 0xF
        words = (c[..., 0::2] | (c[..., 1::2] << 4)).reshape(k // 512, 128, 2 * n)
    return np.ascontiguousarray(words), np.ascontiguousarray(byte.astype(np.uint8).reshape(k // 512, 16, n))


def unpack_weight(words, scales, fmt):
    g, _, n = scales.shape
    words = np.ascontiguousarray(words).reshape(g, 128, n, -1)
    if fmt == "e4m3":
        vals = words.view(ml_dtypes.float8_e4m3fn).astype(np.float64)
    else:
        nib = np.empty((g, 128, n, 4), np.uint8)
        nib[..., 0::2] = words & 0xF
        nib[..., 1::2] = words >> 4
        vals = E2M1[nib]
    vals = vals * np.repeat(np.exp2(scales.astype(np.float64) - 127.0), 8, axis=1)[..., None]
    return vals.transpose(0, 1, 3, 2).reshape(g * 512, n)


def silu(v):
    return v / (1.0 + np.exp(-np.maximum(v, -700.0)))


K, T, E, C, H, N = 512, 512, 4, 256, 512, 512


def by_expert(wq, xq):
    return np.concatenate([wq[e].T @ xq[:, e * C:(e + 1) * C] for e in range(E)], axis=1)


def setup_inputs():
    n = np.random.standard_normal
    s = mx_kscale(K)[:, None]
    u = mx_kscale(H)
    first = np.random.permutation(np.repeat(np.arange(E), T // E))
    second = (first + 1 + np.random.permutation(np.repeat(np.arange(E - 1), -(-T // (E - 1)))[:T])) % E
    while np.bincount(second, minlength=E).max() != T // E:
        load = np.bincount(second, minlength=E); hi, lo = int(load.argmax()), int(load.argmin())
        t = np.flatnonzero((second == hi) & (first != lo))[0]; second[t] = lo
    slot_token = np.empty(E * C, np.int64); pos = np.empty((2, T), np.int64); fill = np.zeros(E, np.int64)
    place = np.stack([np.random.permutation(C) for _ in range(E)])
    for r, deal in enumerate((first, second)):
        for t in np.random.permutation(T):
            e = deal[t]; j = e * C + place[e, fill[e]]; fill[e] += 1; slot_token[j] = t; pos[r, t] = j
    g = np.random.uniform(0.2, 0.8, T)
    w1 = [pack_weight(m, "e2m1") for m in n((E, K, H)) / np.sqrt(K) / s[None]]
    w3 = [pack_weight(m, "e2m1") for m in n((E, K, H)) / np.sqrt(K) / s[None] * u[None, None, :]]
    w2 = [pack_weight(m, "e2m1") for m in n((E, H, N)) / np.sqrt(H) / u[None, :, None]]
    return {
        "xT": (n((K, T)) * s).astype(np.float32),
        "w1_words": np.stack([m[0] for m in w1]),
        "w1_scales": np.stack([m[1] for m in w1]),
        "w3_words": np.stack([m[0] for m in w3]),
        "w3_scales": np.stack([m[1] for m in w3]),
        "w2_words": np.stack([m[0] for m in w2]),
        "w2_scales": np.stack([m[1] for m in w2]),
        "gate": np.stack([np.tile(g, (N, 1)), np.tile(1.0 - g, (N, 1))]).astype(np.float32),
        "offs": striped(slot_token),
        "pos1": striped(pos[0]),
        "pos2": striped(pos[1]),
    }


def reference(xT, w1_words, w1_scales, w3_words, w3_scales, w2_words, w2_scales, gate, offs, pos1, pos2):
    idx = unstriped(offs)
    w1 = np.stack([unpack_weight(w1_words[e], w1_scales[e], "e2m1") for e in range(E)])
    w3 = np.stack([unpack_weight(w3_words[e], w3_scales[e], "e2m1") for e in range(E)])
    w2 = np.stack([unpack_weight(w2_words[e], w2_scales[e], "e2m1") for e in range(E)])
    xq = mxq(f64(xT)[:, idx], 0, "e4m3")
    h = silu(by_expert(w1, xq))
    h = h * by_expert(w3, xq)
    y = by_expert(w2, mxq(h, 0, "e4m3"))
    return f64(gate[0]) * y[:, unstriped(pos1)] + f64(gate[1]) * y[:, unstriped(pos2)]

@@ -1,0 +1,233 @@
+from contextlib import ExitStack
+
+import concourse.mybir as mybir
+from concourse.masks import make_identity
+
+F32 = mybir.dt.float32
+BF16 = mybir.dt.bfloat16
+I32 = mybir.dt.int32
+U32 = mybir.dt.uint32
+U16 = mybir.dt.uint16
+U8 = mybir.dt.uint8
+FP8X4 = mybir.dt.float8_e4m3fn_x4
+FP4X4 = mybir.dt.float4_e2m1fn_x4
+ADD, MULT = mybir.AluOpType.add, mybir.AluOpType.mult
+SILU = mybir.ActivationFunctionType.Silu
+
+P = 128
+K, T, E, C, H, N = 512, 512, 4, 256, 512, 512
+S = E * C
+PACK = 4
+UNIT = 128
+X_SCALAR = 44
+
+FLOPS = 2 * S * (2 * K * H + H * N)
+
+
+def tile_moe_pln_glu_silu_kernel(
+    tc, xT, w1_words, w1_scales, w3_words, w3_scales, w2_words, w2_scales, gate, offs, pos1, pos2, out
+):
+    nc = tc.nc
+    with ExitStack() as ctx:
+        keep = ctx.enter_context(tc.tile_pool(name="keep", bufs=1))
+        work = ctx.enter_context(tc.tile_pool(name="work", bufs=4))
+        psum = ctx.enter_context(tc.psum_pool(name="psum", bufs=1))
+
+        planes = [keep.tile([P, E * H], U8, name=f"plane{i}", align_bytes=64) for i in range(3)]
+        words = [keep.tile([P, E, 2 * H], U8, name=f"words{i}", align_bytes=64) for i in range(3)]
+
+        def load_words(engine, i, dram, e0, e1):
+            engine.dma_start(
+                words[i][:, e0:e1, :].bitcast(I32),
+                dram.bitcast(I32)[e0:e1].rearrange("e o p n -> p (e o) n"),
+            )
+
+        def load_scales(engines, i, dram):
+            rows = dram.bitcast(I32).rearrange("e o (q r) n -> r q (e o) n", r=4)
+            plane = planes[i][:].bitcast(I32).rearrange("p (e n) -> p e n", e=E)
+            for r in range(4):
+                engines[r].dma_start(plane[r:P:32], rows[r])
+
+        warm = keep.tile([P, 1], F32, name="warm")
+        nc.vector.memset(warm[:], 0.0)
+        offs_sb = keep.tile([P, S // 16], U16, name="offs_sb")
+        x_rows = xT.rearrange("(p j) t -> p j t", j=PACK)
+        X_CUTS = (0, 384, T)
+        x_raw, x_bf = [], []
+        for h in range(2):
+            n = X_CUTS[h + 1] - X_CUTS[h]
+            x_raw.append(keep.tile([P, PACK, n], F32, name=f"x_raw{h}", align_bytes=64))
+            x_bf.append(keep.tile([P, n, PACK], BF16, name=f"x_bf{h}", align_bytes=64))
+        nc.sync.dma_start(offs_sb[:], offs)
+        for h in range(2):
+            nc.sync.dma_start(x_raw[h][:], x_rows[:, :, X_CUTS[h] : X_CUTS[h + 1]])
+
+        x_scales = keep.tile([P, T], U8, name="x_scales", align_bytes=64)
+        nc.gpsimd.memset(x_scales[:], 0)
+        for i in (0, 1):
+            nc.vector.memset(planes[i][:].bitcast(I32), 0)
+        load_words(nc.gpsimd, 0, w1_words, 0, 1)
+        load_words(nc.gpsimd, 1, w3_words, 0, 1)
+        load_scales([nc.scalar] * 4, 0, w1_scales)
+        load_scales([nc.scalar] + [nc.sync] * 3, 1, w3_scales)
+        nc.scalar.activation(warm[:], warm[:], SILU)
+        nc.vector.memset(planes[2][:].bitcast(I32), 0)
+        ident = keep.tile([P, P], F32, name="ident")
+        make_identity(nc, ident[:])
+        load_words(nc.sync, 0, w1_words, 1, 4)
+        load_words(nc.sync, 1, w3_words, 1, 4)
+        load_scales([nc.sync] * 4, 2, w2_scales)
+        load_words(nc.sync, 2, w2_words, 0, 4)
+        pos_sb = []
+        for i, pos in enumerate((pos1, pos2)):
+            pos_tile = keep.tile([P, T // 16], U16, name=f"pos_sb{i}")
+            nc.sync.dma_start(pos_tile[:], pos)
+            pos_sb.append(pos_tile)
+        gates = [keep.tile([P, N // P, T], F32, name=f"gate{i}") for i in range(2)]
+        for i in range(2):
+            nc.sync.dma_start(gates[i][:], gate[i].rearrange("(b p) t -> p b t", p=P))
+
+        x_codes = keep.tile([P, T], U32, name="x_codes", align_bytes=64)
+        for h in range(2):
+            n = X_CUTS[h + 1] - X_CUTS[h]
+            cut = 0 if h == 0 else X_SCALAR
+            src = x_raw[h][:].rearrange("p j t -> p t j")
+            if cut:
+                nc.scalar.copy(x_bf[h][:, 0:cut, :], src[:, 0:cut, :])
+            nc.vector.tensor_copy(x_bf[h][:, cut:n, :], src[:, cut:n, :])
+            for q0, q1 in (((0, 256), (256, 384)) if h == 0 else ((0, 128),)):
+                cols = slice(X_CUTS[h] + q0, X_CUTS[h] + q1)
+                nc.vector.quantize_mx(
+                    out=x_codes[:, cols].bitcast(FP8X4),
+                    scales=x_scales[:, cols],
+                    in_=x_bf[h][:, q0:q1, :].rearrange("p t j -> p (t j)"),
+                )
+
+        CHUNKS = [128,256,256,384]
+        starts = [sum(CHUNKS[:c]) for c in range(len(CHUNKS))]
+        slot_codes = [keep.tile([P, n], U32, name=f"slot_codes{c}", align_bytes=64) for c, n in enumerate(CHUNKS)]
+        slot_scales = [keep.tile([P, n], U8, name=f"slot_scales{c}", align_bytes=64) for c, n in enumerate(CHUNKS)]
+        y_sb = [keep.tile([P, S], F32, name=f"y_sb{b}") for b in range(N // P)]
+        h_codes = [keep.tile([P, C], U32, name=f"h_codes{e}", align_bytes=64) for e in range(E)]
+        h_scales = [keep.tile([P, C], U8, name=f"h_scales{e}", align_bytes=64) for e in range(E)]
+        BANK = {"A0":0,"B0":2,"T0":6,"A1":1,"B1":3,"T1":4,"A2":0,"B2":2,"T2":5,"A3":1,"B3":3,"T3":7,"A4":0,"B4":2,"T4":7,"A5":1,"B5":3,"T5":6,"A6":0,"B6":2,"T6":1,"A7":1,"B7":3,"T7":0,"Yp0":7,"Yp1":6,"Yp2":4,"Yp3":2,"Yq0":5,"Yr0":1,"Yq1":0,"Yq2":7,"Yq3":3}
+        ENG = {"yop1":"S","tc5":"S","yop0":"S","yop2":"S","tc1":"S","tc4":"S","tc0":"S","tc3":"S","tc6":"S","tc7":"V","yor0":"V","tc2":"S","yoq3":"S","yoq1":"S","yoq0":"V","yoq2":"S","yop3":"S"}
+        GROUPS = {"p0": ([0,1], 0), "p1": ([0,1], 1), "p2": ([0,1], 2), "p3": ([0,1], 3), "q0": ([2], 0), "r0": ([3], 0), "q1": ([2,3], 1), "q2": ([2,3], 2), "q3": ([2,3], 3)}
+        tiles = {}
+
+        def copier(n):
+            return nc.vector.tensor_copy if ENG.get(n) == "V" else nc.scalar.copy
+
+        def gather(kind, c):
+            lst = offs_sb[:, starts[c] // 16 : (starts[c] + CHUNKS[c]) // 16]
+            if kind == "w":
+                nc.vector.tensor_copy(slot_codes[c][:], x_codes[:].indirect(lst))
+            else:
+                nc.vector.tensor_copy(slot_scales[c][:], x_scales[:].indirect(lst))
+
+        def layer1(i, u):
+            e = u // 2
+            c = max(k for k in range(len(CHUNKS)) if starts[k] <= u * UNIT)
+            cols = slice(u * UNIT - starts[c], (u + 1) * UNIT - starts[c])
+            key = f"{'AB'[i]}{u}"
+            bank = psum.tile([P, H], F32, name="acc", tag=f"bank{BANK[key]}")
+            nc.tensor.matmul_mx(
+                out=bank[:],
+                lhsT=slot_codes[c][:, cols].bitcast(FP8X4),
+                lhsT_scale=slot_scales[c][:, cols],
+                rhs=words[i][:, e, :].bitcast(FP4X4),
+                rhs_scale=planes[i][:, e * H : (e + 1) * H],
+                start=True,
+                stop=True,
+            )
+            tiles[key] = bank
+
+        def silu(u):
+            act = work.tile([P, H], F32, name="act")
+            nc.scalar.activation(act[:], tiles[f"A{u}"][:], SILU)
+            tiles["act", u] = act
+
+        def product(u):
+            hid = work.tile([P, H], BF16, name="hid")
+            nc.vector.tensor_tensor(hid[:], tiles["act", u][:], tiles[f"B{u}"][:], MULT)
+            tiles["hid", u] = hid
+
+        def turn(u):
+            pairs = tiles["hid", u][:].bitcast(F32)
+            turned = psum.tile([P, 2, UNIT], F32, name="turned", tag=f"bank{BANK[f'T{u}']}")
+            for k in range(2):
+                nc.tensor.transpose(turned[:, k, :], pairs[:, k : H // 2 : 2], ident[:])
+            tiles["turned", u] = turned
+
+        def turned_out(u):
+            hid_k = work.tile([P, UNIT * PACK], BF16, name="hid_k", align_bytes=64)
+            copier(f"tc{u}")(
+                hid_k[:].bitcast(F32).rearrange("p (s u) -> p s u", u=2),
+                tiles["turned", u][:].rearrange("p u s -> p s u"),
+            )
+            tiles["hid_k", u] = hid_k
+
+        def quant(u):
+            e, cols = u // 2, slice(u % 2 * UNIT, (u % 2 + 1) * UNIT)
+            nc.vector.quantize_mx(
+                out=h_codes[e][:, cols].bitcast(FP8X4), scales=h_scales[e][:, cols], in_=tiles["hid_k", u][:]
+            )
+
+        def layer2(g, e):
+            es, b = GROUPS[g]
+            if ("y", g) not in tiles:
+                tiles["y", g] = psum.tile([P, len(es) * C], F32, name="acc_y", tag=f"bank{BANK['Y' + g]}")
+            n0, c0 = b * P, es.index(e) * C
+            nc.tensor.matmul_mx(
+                out=tiles["y", g][:, c0 : c0 + C],
+                lhsT=words[2][:, e, 2 * n0 : 2 * (n0 + P)].bitcast(FP4X4),
+                lhsT_scale=planes[2][:, e * N + n0 : e * N + n0 + P],
+                rhs=h_codes[e][:].bitcast(FP8X4),
+                rhs_scale=h_scales[e][:],
+                start=True,
+                stop=True,
+            )
+
+        def y_out(g):
+            es, b = GROUPS[g]
+            copier("yo" + g)(y_sb[b][:, es[0] * C : (es[-1] + 1) * C], tiles["y", g][:])
+
+        def picked(b, i):
+            part = work.tile([P, T], F32, name=f"part{i}")
+            nc.vector.tensor_tensor(part[:], y_sb[b][:].indirect(pos_sb[i][:]), gates[i][:, b, :], MULT)
+            tiles["part", b, i] = part
+
+        def add(b):
+            res = work.tile([P, T], F32, name="res")
+            cuts = (0, 256, T) if b == N // P - 1 else (0, T)
+            for t0, t1 in zip(cuts[:-1], cuts[1:]):
+                cols = slice(t0, t1)
+                nc.vector.tensor_tensor(res[:, cols], tiles["part", b, 0][:, cols], tiles["part", b, 1][:, cols], ADD)
+                nc.sync.dma_start(out[b * P : (b + 1) * P, cols], res[:, cols])
+
+        for n in ("gs0 gw0 gs2 gs1 gw1 a0 gw2 b0 a1 silu0 b1 a2 M0 silu1 T0 gs3 b2 silu2 tc0 M1 gw3 a3 a4 b3 silu3 M2 T1 silu4 tc1 a5 b4 silu5 M3 a6 Q1 b5 M4 T3 a7 b6 silu6 M5 T2 tc3 silu7 b7 Q0 tc2 T5 M6 T4 M7 Q2 Q3 T6 yp3.0 tc5 Q5 tc4 T7 yp3.1 Q4 yp1.0 yp0.1 tc6 yop3 tc7 yp0.0 yq0.2 Q6 yop0 yq3.2 yp1.1 Q7 yr0.3 yq3.3 yp2.1 yoq0 yq1.3 yp2.0 yor0 yop1 c01 yq2.2 yoq3 c00 yq2.3 yq1.2 c31 yoq2 yoq1 c30 c10 c11 yop2 add3 c21 c20 add1 add0 add2").split():
+            k = int(n[-1])
+            if n.startswith("gw") or n.startswith("gs"):
+                gather(n[1], k)
+            elif n.startswith("silu"):
+                silu(k)
+            elif n.startswith("tc"):
+                turned_out(k)
+            elif n.startswith("yo"):
+                y_out(n[2:])
+            elif n.startswith("add"):
+                add(k)
+            elif n[0:1] == "a":
+                layer1(0, k)
+            elif n[0:1] == "b":
+                layer1(1, k)
+            elif n[0:1] == "M":
+                product(k)
+            elif n[0:1] == "T":
+                turn(k)
+            elif n[0:1] == "Q":
+                quant(k)
+            elif n[0:1] == "y":
+                layer2(n[1:-2], k)
+            elif n[0:1] == "c":
+                picked(int(n[1]), k)

@@ -31,6 +31,7 @@ def tile_moe_pln_glu_silu_kernel(
     with ExitStack() as ctx:
         keep = ctx.enter_context(tc.tile_pool(name="keep", bufs=1))
         work = ctx.enter_context(tc.tile_pool(name="work", bufs=4))
+        turn_pool = ctx.enter_context(tc.tile_pool(name="turn_pool", bufs=8))
         psum = ctx.enter_context(tc.psum_pool(name="psum", bufs=1))
 
         planes = [keep.tile([P, E * H], U8, name=f"plane{i}", align_bytes=64) for i in range(3)]
@@ -52,24 +53,24 @@ def tile_moe_pln_glu_silu_kernel(
         nc.vector.memset(warm[:], 0.0)
         offs_sb = keep.tile([P, S // 16], U16, name="offs_sb")
         x_rows = xT.rearrange("(p j) t -> p j t", j=PACK)
-        X_CUTS = (0, 384, T)
+        X_CUTS = (0, 256, T)
         x_raw, x_bf = [], []
         for h in range(2):
             n = X_CUTS[h + 1] - X_CUTS[h]
             x_raw.append(keep.tile([P, PACK, n], F32, name=f"x_raw{h}", align_bytes=64))
             x_bf.append(keep.tile([P, n, PACK], BF16, name=f"x_bf{h}", align_bytes=64))
-        nc.sync.dma_start(offs_sb[:], offs)
+
         for h in range(2):
             nc.sync.dma_start(x_raw[h][:], x_rows[:, :, X_CUTS[h] : X_CUTS[h + 1]])
-
+        nc.sync.dma_start(offs_sb[:], offs)
         x_scales = keep.tile([P, T], U8, name="x_scales", align_bytes=64)
         nc.gpsimd.memset(x_scales[:], 0)
         for i in (0, 1):
             nc.vector.memset(planes[i][:].bitcast(I32), 0)
-        load_words(nc.gpsimd, 0, w1_words, 0, 1)
-        load_words(nc.gpsimd, 1, w3_words, 0, 1)
-        load_scales([nc.scalar] * 4, 0, w1_scales)
-        load_scales([nc.scalar] + [nc.sync] * 3, 1, w3_scales)
+        load_words(nc.sync, 0, w1_words, 0, 1)
+        load_words(nc.sync, 1, w3_words, 0, 1)
+        load_scales([nc.scalar] * 3 + [nc.sync], 0, w1_scales)
+        load_scales([nc.sync] * 4, 1, w3_scales)
         nc.scalar.activation(warm[:], warm[:], SILU)
         nc.vector.memset(planes[2][:].bitcast(I32), 0)
         ident = keep.tile([P, P], F32, name="ident")
@@ -90,12 +91,12 @@ def tile_moe_pln_glu_silu_kernel(
         x_codes = keep.tile([P, T], U32, name="x_codes", align_bytes=64)
         for h in range(2):
             n = X_CUTS[h + 1] - X_CUTS[h]
-            cut = 0 if h == 0 else X_SCALAR
+            cut = 96 if h == 0 else X_SCALAR
             src = x_raw[h][:].rearrange("p j t -> p t j")
             if cut:
                 nc.scalar.copy(x_bf[h][:, 0:cut, :], src[:, 0:cut, :])
             nc.vector.tensor_copy(x_bf[h][:, cut:n, :], src[:, cut:n, :])
-            for q0, q1 in (((0, 256), (256, 384)) if h == 0 else ((0, 128),)):
+            for q0, q1 in ((0, n),):
                 cols = slice(X_CUTS[h] + q0, X_CUTS[h] + q1)
                 nc.vector.quantize_mx(
                     out=x_codes[:, cols].bitcast(FP8X4),
@@ -103,17 +104,18 @@ def tile_moe_pln_glu_silu_kernel(
                     in_=x_bf[h][:, q0:q1, :].rearrange("p t j -> p (t j)"),
                 )
 
-        CHUNKS = [128,256,256,384]
+        CHUNKS = [128,384,384,128]
         starts = [sum(CHUNKS[:c]) for c in range(len(CHUNKS))]
         slot_codes = [keep.tile([P, n], U32, name=f"slot_codes{c}", align_bytes=64) for c, n in enumerate(CHUNKS)]
         slot_scales = [keep.tile([P, n], U8, name=f"slot_scales{c}", align_bytes=64) for c, n in enumerate(CHUNKS)]
         y_sb = [keep.tile([P, S], F32, name=f"y_sb{b}") for b in range(N // P)]
         h_codes = [keep.tile([P, C], U32, name=f"h_codes{e}", align_bytes=64) for e in range(E)]
         h_scales = [keep.tile([P, C], U8, name=f"h_scales{e}", align_bytes=64) for e in range(E)]
-        BANK = {"A0":0,"B0":2,"T0":6,"A1":1,"B1":3,"T1":4,"A2":0,"B2":2,"T2":5,"A3":1,"B3":3,"T3":7,"A4":0,"B4":2,"T4":7,"A5":1,"B5":3,"T5":6,"A6":0,"B6":2,"T6":1,"A7":1,"B7":3,"T7":0,"Yp0":7,"Yp1":6,"Yp2":4,"Yp3":2,"Yq0":5,"Yr0":1,"Yq1":0,"Yq2":7,"Yq3":3}
-        ENG = {"yop1":"S","tc5":"S","yop0":"S","yop2":"S","tc1":"S","tc4":"S","tc0":"S","tc3":"S","tc6":"S","tc7":"V","yor0":"V","tc2":"S","yoq3":"S","yoq1":"S","yoq0":"V","yoq2":"S","yop3":"S"}
+        BANK = {"A0":0,"B0":2,"T0":4,"A1":1,"B1":3,"T1":4,"A2":0,"B2":2,"T2":7,"A3":1,"B3":3,"T3":5,"A4":0,"B4":2,"T4":4,"A5":1,"B5":3,"T5":1,"A6":0,"B6":2,"T6":2,"A7":1,"B7":3,"T7":0,"Yp0":6,"Yp1":5,"Yp2":2,"Yp3":1,"Yq0":4,"Yr0":3,"Yq1":4,"Yq2":0,"Yq3":7}
+        ENG = {"yor0":"V","tc4":"S","yoq0":"S","tc7":"S","tc3":"S","tc5":"S","tc1":"S","yop1":"S","tc2":"S","yop2":"S","yop3":"S","tc6":"S","yoq2":"S","yop0":"V","yoq1":"S","tc0":"S","yoq3":"S"}
         GROUPS = {"p0": ([0,1], 0), "p1": ([0,1], 1), "p2": ([0,1], 2), "p3": ([0,1], 3), "q0": ([2], 0), "r0": ([3], 0), "q1": ([2,3], 1), "q2": ([2,3], 2), "q3": ([2,3], 3)}
         tiles = {}
+        QPAIR = [0,1,2]
 
         def copier(n):
             return nc.vector.tensor_copy if ENG.get(n) == "V" else nc.scalar.copy
@@ -160,17 +162,25 @@ def tile_moe_pln_glu_silu_kernel(
             tiles["turned", u] = turned
 
         def turned_out(u):
-            hid_k = work.tile([P, UNIT * PACK], BF16, name="hid_k", align_bytes=64)
+            e, s = u // 2, u % 2
+            pair = e in QPAIR
+            if not pair or ("hid_k", e) not in tiles:
+                hid_k = turn_pool.tile([P, (2 if pair else 1) * UNIT * PACK], BF16, name="hid_k", align_bytes=64)
+                tiles["hid_k", e if pair else f"u{u}"] = hid_k
+            hid_k = tiles["hid_k", e if pair else f"u{u}"]
+            part = hid_k[:, s * UNIT * PACK : (s + 1) * UNIT * PACK] if pair else hid_k[:]
             copier(f"tc{u}")(
-                hid_k[:].bitcast(F32).rearrange("p (s u) -> p s u", u=2),
+                part.bitcast(F32).rearrange("p (s u) -> p s u", u=2),
                 tiles["turned", u][:].rearrange("p u s -> p s u"),
             )
-            tiles["hid_k", u] = hid_k
 
         def quant(u):
-            e, cols = u // 2, slice(u % 2 * UNIT, (u % 2 + 1) * UNIT)
+            e = u // 2
+            cols = slice(0, C) if e in QPAIR else slice(u % 2 * UNIT, (u % 2 + 1) * UNIT)
             nc.vector.quantize_mx(
-                out=h_codes[e][:, cols].bitcast(FP8X4), scales=h_scales[e][:, cols], in_=tiles["hid_k", u][:]
+                out=h_codes[e][:, cols].bitcast(FP8X4),
+                scales=h_scales[e][:, cols],
+                in_=tiles["hid_k", e if e in QPAIR else f"u{u}"][:],
             )
 
         def layer2(g, e):
@@ -193,19 +203,20 @@ def tile_moe_pln_glu_silu_kernel(
             copier("yo" + g)(y_sb[b][:, es[0] * C : (es[-1] + 1) * C], tiles["y", g][:])
 
         def picked(b, i):
-            part = work.tile([P, T], F32, name=f"part{i}")
-            nc.vector.tensor_tensor(part[:], y_sb[b][:].indirect(pos_sb[i][:]), gates[i][:, b, :], MULT)
+            part_tile = work.tile([P, T], F32, name=f"part{i}")
+            part = part_tile[:]
+            nc.vector.tensor_tensor(part, y_sb[b][:].indirect(pos_sb[i][:]), gates[i][:, b, :], MULT)
             tiles["part", b, i] = part
 
         def add(b):
             res = work.tile([P, T], F32, name="res")
-            cuts = (0, 256, T) if b == N // P - 1 else (0, T)
+            cuts = (0, 384, T) if b == 3 else (0, T)
             for t0, t1 in zip(cuts[:-1], cuts[1:]):
                 cols = slice(t0, t1)
                 nc.vector.tensor_tensor(res[:, cols], tiles["part", b, 0][:, cols], tiles["part", b, 1][:, cols], ADD)
                 nc.sync.dma_start(out[b * P : (b + 1) * P, cols], res[:, cols])
 
-        for n in ("gs0 gw0 gs2 gs1 gw1 a0 gw2 b0 a1 silu0 b1 a2 M0 silu1 T0 gs3 b2 silu2 tc0 M1 gw3 a3 a4 b3 silu3 M2 T1 silu4 tc1 a5 b4 silu5 M3 a6 Q1 b5 M4 T3 a7 b6 silu6 M5 T2 tc3 silu7 b7 Q0 tc2 T5 M6 T4 M7 Q2 Q3 T6 yp3.0 tc5 Q5 tc4 T7 yp3.1 Q4 yp1.0 yp0.1 tc6 yop3 tc7 yp0.0 yq0.2 Q6 yop0 yq3.2 yp1.1 Q7 yr0.3 yq3.3 yp2.1 yoq0 yq1.3 yp2.0 yor0 yop1 c01 yq2.2 yoq3 c00 yq2.3 yq1.2 c31 yoq2 yoq1 c30 c10 c11 yop2 add3 c21 c20 add1 add0 add2").split():
+        for n in ("gs0 gw0 a0 gs1 gw1 b0 a1 b1 silu0 gw2 silu1 M0 gs2 M1 a2 b2 T0 a3 silu2 a4 tc0 gs3 silu3 M2 silu4 b3 T1 M3 a5 tc1 gw3 b4 a6 silu5 M4 b5 T3 a7 b6 T4 silu6 silu7 M5 tc3 M6 b7 M7 T5 T2 tc4 tc5 Q1 Q5 T6 T7 tc2 tc6 tc7 Q3 yp1.0 Q6 Q7 yp0.0 yp3.0 yq0.2 yp0.1 yp3.1 yoq0 yq3.2 yop0 yp1.1 yr0.3 yor0 c00 yq2.3 yq1.3 yq2.2 yop3 yq3.3 yop1 yq1.2 yoq1 yp2.1 yp2.0 yoq2 c01 c11 yop2 yoq3 c10 add0 c21 add1 c20 c31 c30 add2 add3").split():
             k = int(n[-1])
             if n.startswith("gw") or n.startswith("gs"):
                 gather(n[1], k)

@@ -30,7 +30,7 @@ def tile_moe_pln_glu_silu_kernel(
     nc = tc.nc
     with ExitStack() as ctx:
         keep = ctx.enter_context(tc.tile_pool(name="keep", bufs=1))
-        work = ctx.enter_context(tc.tile_pool(name="work", bufs=4))
+        work = ctx.enter_context(tc.tile_pool(name="work", bufs=8))
         turn_pool = ctx.enter_context(tc.tile_pool(name="turn_pool", bufs=8))
         psum = ctx.enter_context(tc.psum_pool(name="psum", bufs=1))
 
@@ -111,8 +111,8 @@ def tile_moe_pln_glu_silu_kernel(
         y_sb = [keep.tile([P, S], F32, name=f"y_sb{b}") for b in range(N // P)]
         h_codes = [keep.tile([P, C], U32, name=f"h_codes{e}", align_bytes=64) for e in range(E)]
         h_scales = [keep.tile([P, C], U8, name=f"h_scales{e}", align_bytes=64) for e in range(E)]
-        BANK = {"A0":0,"B0":2,"T0":4,"A1":1,"B1":3,"T1":4,"A2":0,"B2":2,"T2":7,"A3":1,"B3":3,"T3":5,"A4":0,"B4":2,"T4":4,"A5":1,"B5":3,"T5":1,"A6":0,"B6":2,"T6":2,"A7":1,"B7":3,"T7":0,"Yp0":6,"Yp1":5,"Yp2":2,"Yp3":1,"Yq0":4,"Yr0":3,"Yq1":4,"Yq2":0,"Yq3":7}
-        ENG = {"yor0":"V","tc4":"S","yoq0":"S","tc7":"S","tc3":"S","tc5":"S","tc1":"S","yop1":"S","tc2":"S","yop2":"S","yop3":"S","tc6":"S","yoq2":"S","yop0":"V","yoq1":"S","tc0":"S","yoq3":"S"}
+        BANK = {"A0":7,"B0":5,"T0":6,"A1":2,"B1":7,"T1":1,"A2":6,"B2":0,"T2":2,"A3":3,"B3":1,"T3":4,"A4":2,"B4":4,"T4":6,"A5":6,"B5":0,"T5":0,"A6":3,"B6":7,"T6":1,"A7":5,"B7":3,"T7":3,"Yp0":6,"Yq0":2,"Yr0":5,"Yp1":2,"Yq1":0,"Yp2":4,"Yq2":3,"Yp3":6,"Yq3":7}
+        ENG = {"tc6":"S","tc4":"V","yoq1":"S","yop1":"S","yoq0":"V","yoq2":"S","yop3":"S","yor0":"S","tc7":"S","yop0":"S","yoq3":"S","tc5":"S","yop2":"S"}
         GROUPS = {"p0": ([0,1], 0), "p1": ([0,1], 1), "p2": ([0,1], 2), "p3": ([0,1], 3), "q0": ([2], 0), "r0": ([3], 0), "q1": ([2,3], 1), "q2": ([2,3], 2), "q3": ([2,3], 3)}
         tiles = {}
         QPAIR = [0,1,2]
@@ -216,7 +216,7 @@ def tile_moe_pln_glu_silu_kernel(
                 nc.vector.tensor_tensor(res[:, cols], tiles["part", b, 0][:, cols], tiles["part", b, 1][:, cols], ADD)
                 nc.sync.dma_start(out[b * P : (b + 1) * P, cols], res[:, cols])
 
-        for n in ("gs0 gw0 a0 gs1 gw1 b0 a1 b1 silu0 gw2 silu1 M0 gs2 M1 a2 b2 T0 a3 silu2 a4 tc0 gs3 silu3 M2 silu4 b3 T1 M3 a5 tc1 gw3 b4 a6 silu5 M4 b5 T3 a7 b6 T4 silu6 silu7 M5 tc3 M6 b7 M7 T5 T2 tc4 tc5 Q1 Q5 T6 T7 tc2 tc6 tc7 Q3 yp1.0 Q6 Q7 yp0.0 yp3.0 yq0.2 yp0.1 yp3.1 yoq0 yq3.2 yop0 yp1.1 yr0.3 yor0 c00 yq2.3 yq1.3 yq2.2 yop3 yq3.3 yop1 yq1.2 yoq1 yp2.1 yp2.0 yoq2 c01 c11 yop2 yoq3 c10 add0 c21 add1 c20 c31 c30 add2 add3").split():
+        for n in ("gs0 gw0 gs1 gw1 gs2 gw2 gs3 gw3 a0 silu0 a1 silu1 a2 b0 silu2 a3 b1 silu3 a4 b2 silu4 M0 a5 b3 silu5 M1 a6 b4 silu6 M2 a7 b5 silu7 M3 T0 b6 M4 T1 b7 M5 T2 M6 T3 tc0 M7 T4 tc1 T5 tc2 T6 tc3 T7 tc4 tc5 tc6 tc7 Q1 Q3 Q5 Q6 Q7 yp0.0 yp0.1 yq0.2 yop0 yr0.3 yoq0 yq1.2 yq1.3 yor0 yp2.0 yp2.1 yoq1 yp1.0 yp1.1 yop2 yp3.0 yp3.1 yop1 yq3.2 yq3.3 yop3 yq2.2 yq2.3 yoq3 yoq2 c00 c01 c10 add0 c11 c20 add1 c21 c30 add2 c31 add3").split():
             k = int(n[-1])
             if n.startswith("gw") or n.startswith("gs"):
                 gather(n[1], k)

@@ -19,7 +19,20 @@ K, T, E, C, H, N = 512, 512, 4, 256, 512, 512
 S = E * C
 PACK = 4
 UNIT = 128
-X_SCALAR = 44
+UNITS = S // UNIT
+UNITS_PER_EXPERT = C // UNIT
+BLOCKS = N // P
+LIST_ROWS = 16
+PSUM_BANKS = 8
+
+HALF = T // 2
+X_ON_SCALAR = 96
+GATHER_CUTS = (0, 256, 640, 1024)
+ON_GPSIMD = (0,)
+TURNED_OUT_ON_VECTOR = (4,)
+LAST = E - 1
+RESULTS = ((0, (0, 1)), (0, (2,)), (0, (3,))) + tuple((b, es) for b in range(1, BLOCKS) for es in ((0, 1), (2, 3)))
+LAST_SUM_CUTS = (0, 384, T)
 
 FLOPS = 2 * S * (2 * K * H + H * N)
 
@@ -31,214 +44,200 @@ def tile_moe_pln_glu_silu_kernel(
     with ExitStack() as ctx:
         keep = ctx.enter_context(tc.tile_pool(name="keep", bufs=1))
         work = ctx.enter_context(tc.tile_pool(name="work", bufs=8))
-        turn_pool = ctx.enter_context(tc.tile_pool(name="turn_pool", bufs=8))
-        psum = ctx.enter_context(tc.psum_pool(name="psum", bufs=1))
+        psum = ctx.enter_context(tc.psum_pool(name="psum", bufs=PSUM_BANKS))
 
-        planes = [keep.tile([P, E * H], U8, name=f"plane{i}", align_bytes=64) for i in range(3)]
-        words = [keep.tile([P, E, 2 * H], U8, name=f"words{i}", align_bytes=64) for i in range(3)]
+        def bank(shape):
+            return psum.tile(shape, F32, name="bank")
 
-        def load_words(engine, i, dram, e0, e1):
-            engine.dma_start(
-                words[i][:, e0:e1, :].bitcast(I32),
-                dram.bitcast(I32)[e0:e1].rearrange("e o p n -> p (e o) n"),
+        words = [keep.tile([P, E, 2 * H], U8, name=f"words{m}", align_bytes=64) for m in range(3)]
+        planes = [keep.tile([P, E, H], U8, name=f"planes{m}", align_bytes=64) for m in range(3)]
+
+        def zero_planes(m):
+            nc.vector.memset(planes[m][:].rearrange("p e i -> p (e i)").bitcast(I32), 0)
+
+        def load_words(m, dram, e0, e1):
+            nc.sync.dma_start(
+                words[m][:, e0:e1, :].bitcast(I32), dram.bitcast(I32)[e0:e1].rearrange("e o p i -> p (e o) i")
             )
 
-        def load_scales(engines, i, dram):
-            rows = dram.bitcast(I32).rearrange("e o (q r) n -> r q (e o) n", r=4)
-            plane = planes[i][:].bitcast(I32).rearrange("p (e n) -> p e n", e=E)
-            for r in range(4):
-                engines[r].dma_start(plane[r:P:32], rows[r])
+        def load_scales(engines, m, dram):
+            rows = dram.bitcast(I32).rearrange("e o (Q r) i -> r Q (e o) i", r=4)
+            for r, engine in enumerate(engines):
+                engine.dma_start(planes[m][:].bitcast(I32)[r : P : 32], rows[r])
 
-        warm = keep.tile([P, 1], F32, name="warm")
-        nc.vector.memset(warm[:], 0.0)
-        offs_sb = keep.tile([P, S // 16], U16, name="offs_sb")
-        x_rows = xT.rearrange("(p j) t -> p j t", j=PACK)
-        X_CUTS = (0, 256, T)
-        x_raw, x_bf = [], []
+        x_raw = [keep.tile([P, PACK, HALF], F32, name=f"x_raw{h}", align_bytes=64) for h in range(2)]
         for h in range(2):
-            n = X_CUTS[h + 1] - X_CUTS[h]
-            x_raw.append(keep.tile([P, PACK, n], F32, name=f"x_raw{h}", align_bytes=64))
-            x_bf.append(keep.tile([P, n, PACK], BF16, name=f"x_bf{h}", align_bytes=64))
-
-        for h in range(2):
-            nc.sync.dma_start(x_raw[h][:], x_rows[:, :, X_CUTS[h] : X_CUTS[h + 1]])
+            nc.sync.dma_start(x_raw[h][:], xT.rearrange("(p j) t -> p j t", j=PACK)[:, :, h * HALF : (h + 1) * HALF])
+        offs_sb = keep.tile([P, S // LIST_ROWS], U16, name="offs_sb")
         nc.sync.dma_start(offs_sb[:], offs)
+
         x_scales = keep.tile([P, T], U8, name="x_scales", align_bytes=64)
         nc.gpsimd.memset(x_scales[:], 0)
-        for i in (0, 1):
-            nc.vector.memset(planes[i][:].bitcast(I32), 0)
-        load_words(nc.sync, 0, w1_words, 0, 1)
-        load_words(nc.sync, 1, w3_words, 0, 1)
-        load_scales([nc.scalar] * 3 + [nc.sync], 0, w1_scales)
+        warm = keep.tile([P, 1], F32, name="warm")
+        nc.vector.memset(warm[:], 0.0)
+        zero_planes(0)
+        zero_planes(1)
+        load_words(0, w1_words, 0, 1)
+        load_words(1, w3_words, 0, 1)
+        load_scales([nc.scalar, nc.scalar, nc.scalar, nc.sync], 0, w1_scales)
         load_scales([nc.sync] * 4, 1, w3_scales)
         nc.scalar.activation(warm[:], warm[:], SILU)
-        nc.vector.memset(planes[2][:].bitcast(I32), 0)
+        zero_planes(2)
         ident = keep.tile([P, P], F32, name="ident")
         make_identity(nc, ident[:])
-        load_words(nc.sync, 0, w1_words, 1, 4)
-        load_words(nc.sync, 1, w3_words, 1, 4)
+        load_words(0, w1_words, 1, E)
+        load_words(1, w3_words, 1, E)
         load_scales([nc.sync] * 4, 2, w2_scales)
-        load_words(nc.sync, 2, w2_words, 0, 4)
-        pos_sb = []
-        for i, pos in enumerate((pos1, pos2)):
-            pos_tile = keep.tile([P, T // 16], U16, name=f"pos_sb{i}")
-            nc.sync.dma_start(pos_tile[:], pos)
-            pos_sb.append(pos_tile)
-        gates = [keep.tile([P, N // P, T], F32, name=f"gate{i}") for i in range(2)]
-        for i in range(2):
-            nc.sync.dma_start(gates[i][:], gate[i].rearrange("(b p) t -> p b t", p=P))
+        load_words(2, w2_words, 0, E)
+        pos_sb = [keep.tile([P, T // LIST_ROWS], U16, name=f"pos_sb{r}") for r in range(2)]
+        nc.sync.dma_start(pos_sb[0][:], pos1)
+        nc.sync.dma_start(pos_sb[1][:], pos2)
+        gates = [keep.tile([P, BLOCKS, T], F32, name=f"gates{r}") for r in range(2)]
+        for r in range(2):
+            nc.sync.dma_start(gates[r][:], gate[r].rearrange("(b p) t -> p b t", p=P))
 
         x_codes = keep.tile([P, T], U32, name="x_codes", align_bytes=64)
         for h in range(2):
-            n = X_CUTS[h + 1] - X_CUTS[h]
-            cut = 96 if h == 0 else X_SCALAR
-            src = x_raw[h][:].rearrange("p j t -> p t j")
-            if cut:
-                nc.scalar.copy(x_bf[h][:, 0:cut, :], src[:, 0:cut, :])
-            nc.vector.tensor_copy(x_bf[h][:, cut:n, :], src[:, cut:n, :])
-            for q0, q1 in ((0, n),):
-                cols = slice(X_CUTS[h] + q0, X_CUTS[h] + q1)
-                nc.vector.quantize_mx(
-                    out=x_codes[:, cols].bitcast(FP8X4),
-                    scales=x_scales[:, cols],
-                    in_=x_bf[h][:, q0:q1, :].rearrange("p t j -> p (t j)"),
-                )
+            x_bf = keep.tile([P, HALF, PACK], BF16, name=f"x_bf{h}", align_bytes=64)
+            source = x_raw[h][:].rearrange("p j t -> p t j")
+            nc.scalar.copy(x_bf[:, :X_ON_SCALAR, :], source[:, :X_ON_SCALAR, :])
+            nc.vector.tensor_copy(x_bf[:, X_ON_SCALAR:, :], source[:, X_ON_SCALAR:, :])
+            tokens = slice(h * HALF, (h + 1) * HALF)
+            nc.vector.quantize_mx(
+                out=x_codes[:, tokens].bitcast(FP8X4),
+                scales=x_scales[:, tokens],
+                in_=x_bf[:].rearrange("p t j -> p (t j)"),
+            )
 
-        CHUNKS = [128,384,384,128]
-        starts = [sum(CHUNKS[:c]) for c in range(len(CHUNKS))]
-        slot_codes = [keep.tile([P, n], U32, name=f"slot_codes{c}", align_bytes=64) for c, n in enumerate(CHUNKS)]
-        slot_scales = [keep.tile([P, n], U8, name=f"slot_scales{c}", align_bytes=64) for c, n in enumerate(CHUNKS)]
-        y_sb = [keep.tile([P, S], F32, name=f"y_sb{b}") for b in range(N // P)]
+        slot_codes, slot_scales = {}, {}
+        for cut, (s0, s1) in enumerate(zip(GATHER_CUTS[:-1], GATHER_CUTS[1:])):
+            listed = offs_sb[:, s0 // LIST_ROWS : s1 // LIST_ROWS]
+            scales = keep.tile([P, s1 - s0], U8, name=f"slot_scales{cut}", align_bytes=64)
+            codes = keep.tile([P, s1 - s0], U32, name=f"slot_codes{cut}", align_bytes=64)
+            nc.vector.tensor_copy(scales[:], x_scales[:].indirect(listed))
+            nc.vector.tensor_copy(codes[:], x_codes[:].indirect(listed))
+            for s in range(s0, s1, UNIT):
+                slot_codes[s // UNIT] = codes[:, s - s0 : s - s0 + UNIT]
+                slot_scales[s // UNIT] = scales[:, s - s0 : s - s0 + UNIT]
+
         h_codes = [keep.tile([P, C], U32, name=f"h_codes{e}", align_bytes=64) for e in range(E)]
         h_scales = [keep.tile([P, C], U8, name=f"h_scales{e}", align_bytes=64) for e in range(E)]
-        BANK = {"A0":7,"B0":5,"T0":6,"A1":2,"B1":7,"T1":1,"A2":6,"B2":0,"T2":2,"A3":3,"B3":1,"T3":4,"A4":2,"B4":4,"T4":6,"A5":6,"B5":0,"T5":0,"A6":3,"B6":7,"T6":1,"A7":5,"B7":3,"T7":3,"Yp0":6,"Yq0":2,"Yr0":5,"Yp1":2,"Yq1":0,"Yp2":4,"Yq2":3,"Yp3":6,"Yq3":7}
-        ENG = {"tc6":"S","tc4":"V","yoq1":"S","yop1":"S","yoq0":"V","yoq2":"S","yop3":"S","yor0":"S","tc7":"S","yop0":"S","yoq3":"S","tc5":"S","yop2":"S"}
-        GROUPS = {"p0": ([0,1], 0), "p1": ([0,1], 1), "p2": ([0,1], 2), "p3": ([0,1], 3), "q0": ([2], 0), "r0": ([3], 0), "q1": ([2,3], 1), "q2": ([2,3], 2), "q3": ([2,3], 3)}
-        tiles = {}
-        QPAIR = [0,1,2]
+        a_banks, b_banks, act, up, hidden, turned, hidden_k = {}, {}, {}, {}, {}, {}, {}
 
-        def copier(n):
-            return nc.vector.tensor_copy if ENG.get(n) == "V" else nc.scalar.copy
+        def first_product(banks, m, unit):
+            e = unit // UNITS_PER_EXPERT
+            banks[unit] = bank([P, H])
+            nc.tensor.matmul_mx(
+                out=banks[unit][:],
+                lhsT=slot_codes[unit].bitcast(FP8X4),
+                lhsT_scale=slot_scales[unit],
+                rhs=words[m][:, e, :].bitcast(FP4X4),
+                rhs_scale=planes[m][:, e, :],
+                start=True,
+                stop=True,
+            )
 
-        def gather(kind, c):
-            lst = offs_sb[:, starts[c] // 16 : (starts[c] + CHUNKS[c]) // 16]
-            if kind == "w":
-                nc.vector.tensor_copy(slot_codes[c][:], x_codes[:].indirect(lst))
+        def gate_product(unit):
+            first_product(a_banks, 0, unit)
+
+        def up_product(unit):
+            first_product(b_banks, 1, unit)
+
+        def activate(unit):
+            act[unit] = work.tile([P, H], F32, name="act")
+            nc.scalar.activation(act[unit][:], a_banks[unit][:], SILU)
+
+        def copy_up(unit):
+            if unit in ON_GPSIMD:
+                up[unit] = work.tile([P, H], F32, name="up")
+                nc.scalar.copy(up[unit][:], b_banks[unit][:])
+
+        def multiply(unit):
+            hidden[unit] = work.tile([P, H], BF16, name="hidden")
+            if unit in ON_GPSIMD:
+                nc.gpsimd.tensor_tensor(hidden[unit][:], act[unit][:], up[unit][:], MULT)
             else:
-                nc.vector.tensor_copy(slot_scales[c][:], x_scales[:].indirect(lst))
+                nc.vector.tensor_tensor(hidden[unit][:], act[unit][:], b_banks[unit][:], MULT)
 
-        def layer1(i, u):
-            e = u // 2
-            c = max(k for k in range(len(CHUNKS)) if starts[k] <= u * UNIT)
-            cols = slice(u * UNIT - starts[c], (u + 1) * UNIT - starts[c])
-            key = f"{'AB'[i]}{u}"
-            bank = psum.tile([P, H], F32, name="acc", tag=f"bank{BANK[key]}")
-            nc.tensor.matmul_mx(
-                out=bank[:],
-                lhsT=slot_codes[c][:, cols].bitcast(FP8X4),
-                lhsT_scale=slot_scales[c][:, cols],
-                rhs=words[i][:, e, :].bitcast(FP4X4),
-                rhs_scale=planes[i][:, e * H : (e + 1) * H],
-                start=True,
-                stop=True,
-            )
-            tiles[key] = bank
+        def turn(unit):
+            pairs = hidden[unit][:].bitcast(F32)
+            turned[unit] = bank([P, 2, UNIT])
+            for u in range(2):
+                nc.tensor.transpose(turned[unit][:, u, :], pairs[:, u : H // 2 : 2], ident[:])
 
-        def silu(u):
-            act = work.tile([P, H], F32, name="act")
-            nc.scalar.activation(act[:], tiles[f"A{u}"][:], SILU)
-            tiles["act", u] = act
-
-        def product(u):
-            hid = work.tile([P, H], BF16, name="hid")
-            nc.vector.tensor_tensor(hid[:], tiles["act", u][:], tiles[f"B{u}"][:], MULT)
-            tiles["hid", u] = hid
-
-        def turn(u):
-            pairs = tiles["hid", u][:].bitcast(F32)
-            turned = psum.tile([P, 2, UNIT], F32, name="turned", tag=f"bank{BANK[f'T{u}']}")
-            for k in range(2):
-                nc.tensor.transpose(turned[:, k, :], pairs[:, k : H // 2 : 2], ident[:])
-            tiles["turned", u] = turned
-
-        def turned_out(u):
-            e, s = u // 2, u % 2
-            pair = e in QPAIR
-            if not pair or ("hid_k", e) not in tiles:
-                hid_k = turn_pool.tile([P, (2 if pair else 1) * UNIT * PACK], BF16, name="hid_k", align_bytes=64)
-                tiles["hid_k", e if pair else f"u{u}"] = hid_k
-            hid_k = tiles["hid_k", e if pair else f"u{u}"]
-            part = hid_k[:, s * UNIT * PACK : (s + 1) * UNIT * PACK] if pair else hid_k[:]
-            copier(f"tc{u}")(
-                part.bitcast(F32).rearrange("p (s u) -> p s u", u=2),
-                tiles["turned", u][:].rearrange("p u s -> p s u"),
+        def turn_out(unit):
+            e, place = unit // UNITS_PER_EXPERT, unit % UNITS_PER_EXPERT
+            if e == LAST or place == 0:
+                joined = 1 if e == LAST else UNITS_PER_EXPERT
+                hidden_k[unit] = work.tile([P, joined * UNIT * PACK], BF16, name="hidden_k", align_bytes=64)
+            else:
+                hidden_k[unit] = hidden_k[unit - place]
+            s0 = 0 if e == LAST else place * UNIT
+            copy = nc.vector.tensor_copy if unit in TURNED_OUT_ON_VECTOR else nc.scalar.copy
+            copy(
+                hidden_k[unit][:, s0 * PACK : (s0 + UNIT) * PACK].bitcast(F32).rearrange("p (s u) -> p s u", u=2),
+                turned[unit][:].rearrange("p u s -> p s u"),
             )
 
-        def quant(u):
-            e = u // 2
-            cols = slice(0, C) if e in QPAIR else slice(u % 2 * UNIT, (u % 2 + 1) * UNIT)
+        def quantise(unit):
+            e, place = unit // UNITS_PER_EXPERT, unit % UNITS_PER_EXPERT
+            if e == LAST:
+                slots = slice(place * UNIT, (place + 1) * UNIT)
+            elif place == UNITS_PER_EXPERT - 1:
+                slots = slice(0, C)
+            else:
+                return
             nc.vector.quantize_mx(
-                out=h_codes[e][:, cols].bitcast(FP8X4),
-                scales=h_scales[e][:, cols],
-                in_=tiles["hid_k", e if e in QPAIR else f"u{u}"][:],
+                out=h_codes[e][:, slots].bitcast(FP8X4), scales=h_scales[e][:, slots], in_=hidden_k[unit][:]
             )
 
-        def layer2(g, e):
-            es, b = GROUPS[g]
-            if ("y", g) not in tiles:
-                tiles["y", g] = psum.tile([P, len(es) * C], F32, name="acc_y", tag=f"bank{BANK['Y' + g]}")
-            n0, c0 = b * P, es.index(e) * C
-            nc.tensor.matmul_mx(
-                out=tiles["y", g][:, c0 : c0 + C],
-                lhsT=words[2][:, e, 2 * n0 : 2 * (n0 + P)].bitcast(FP4X4),
-                lhsT_scale=planes[2][:, e * N + n0 : e * N + n0 + P],
-                rhs=h_codes[e][:].bitcast(FP8X4),
-                rhs_scale=h_scales[e][:],
-                start=True,
-                stop=True,
-            )
+        stages = (
+            (gate_product, 0),
+            (up_product, 1),
+            (activate, 0),
+            (copy_up, 1),
+            (multiply, 1),
+            (turn, UNITS - 1),
+            (turn_out, UNITS - 1),
+            (quantise, UNITS),
+        )
+        for step in range(2 * UNITS):
+            for stage, lag in stages:
+                if 0 <= step - lag < UNITS:
+                    stage(step - lag)
 
-        def y_out(g):
-            es, b = GROUPS[g]
-            copier("yo" + g)(y_sb[b][:, es[0] * C : (es[-1] + 1) * C], tiles["y", g][:])
+        y_sb = [keep.tile([P, S], F32, name=f"y_sb{b}") for b in range(BLOCKS)]
+        for index, (b, experts) in enumerate(RESULTS):
+            y_bank = bank([P, len(experts) * C])
+            for g, e in enumerate(experts):
+                nc.tensor.matmul_mx(
+                    out=y_bank[:, g * C : (g + 1) * C],
+                    lhsT=words[2][:, e, 2 * b * P : 2 * (b + 1) * P].bitcast(FP4X4),
+                    lhsT_scale=planes[2][:, e, b * P : (b + 1) * P],
+                    rhs=h_codes[e][:].bitcast(FP8X4),
+                    rhs_scale=h_scales[e][:],
+                    start=True,
+                    stop=True,
+                )
+            copy = nc.vector.tensor_copy if index == 0 else nc.scalar.copy
+            copy(y_sb[b][:, experts[0] * C : (experts[-1] + 1) * C], y_bank[:])
 
-        def picked(b, i):
-            part_tile = work.tile([P, T], F32, name=f"part{i}")
-            part = part_tile[:]
-            nc.vector.tensor_tensor(part, y_sb[b][:].indirect(pos_sb[i][:]), gates[i][:, b, :], MULT)
-            tiles["part", b, i] = part
+        parts = {}
 
-        def add(b):
-            res = work.tile([P, T], F32, name="res")
-            cuts = (0, 384, T) if b == 3 else (0, T)
+        def pick(b, r):
+            parts[b, r] = work.tile([P, T], F32, name=f"part{r}")
+            nc.vector.tensor_tensor(parts[b, r][:], y_sb[b][:].indirect(pos_sb[r][:]), gates[r][:, b, :], MULT)
+
+        def add_and_store(b):
+            total = work.tile([P, T], F32, name="total")
+            cuts = LAST_SUM_CUTS if b == BLOCKS - 1 else (0, T)
             for t0, t1 in zip(cuts[:-1], cuts[1:]):
-                cols = slice(t0, t1)
-                nc.vector.tensor_tensor(res[:, cols], tiles["part", b, 0][:, cols], tiles["part", b, 1][:, cols], ADD)
-                nc.sync.dma_start(out[b * P : (b + 1) * P, cols], res[:, cols])
+                nc.vector.tensor_tensor(total[:, t0:t1], parts[b, 0][:, t0:t1], parts[b, 1][:, t0:t1], ADD)
+                nc.sync.dma_start(out[b * P : (b + 1) * P, t0:t1], total[:, t0:t1])
 
-        for n in ("gs0 gw0 gs1 gw1 gs2 gw2 gs3 gw3 a0 silu0 a1 silu1 a2 b0 silu2 a3 b1 silu3 a4 b2 silu4 M0 a5 b3 silu5 M1 a6 b4 silu6 M2 a7 b5 silu7 M3 T0 b6 M4 T1 b7 M5 T2 M6 T3 tc0 M7 T4 tc1 T5 tc2 T6 tc3 T7 tc4 tc5 tc6 tc7 Q1 Q3 Q5 Q6 Q7 yp0.0 yp0.1 yq0.2 yop0 yr0.3 yoq0 yq1.2 yq1.3 yor0 yp2.0 yp2.1 yoq1 yp1.0 yp1.1 yop2 yp3.0 yp3.1 yop1 yq3.2 yq3.3 yop3 yq2.2 yq2.3 yoq3 yoq2 c00 c01 c10 add0 c11 c20 add1 c21 c30 add2 c31 add3").split():
-            k = int(n[-1])
-            if n.startswith("gw") or n.startswith("gs"):
-                gather(n[1], k)
-            elif n.startswith("silu"):
-                silu(k)
-            elif n.startswith("tc"):
-                turned_out(k)
-            elif n.startswith("yo"):
-                y_out(n[2:])
-            elif n.startswith("add"):
-                add(k)
-            elif n[0:1] == "a":
-                layer1(0, k)
-            elif n[0:1] == "b":
-                layer1(1, k)
-            elif n[0:1] == "M":
-                product(k)
-            elif n[0:1] == "T":
-                turn(k)
-            elif n[0:1] == "Q":
-                quant(k)
-            elif n[0:1] == "y":
-                layer2(n[1:-2], k)
-            elif n[0:1] == "c":
-                picked(int(n[1]), k)
+        for b in range(BLOCKS):
+            pick(b, 0)
+            if b > 0:
+                add_and_store(b - 1)
+            pick(b, 1)
+        add_and_store(BLOCKS - 1)

@@ -31,8 +31,8 @@ GATHER_CUTS = (0, 256, 640, 1024)
 ON_GPSIMD = (0,)
 TURNED_OUT_ON_VECTOR = (4,)
 LAST = E - 1
-RESULTS = ((0, (0, 1)), (0, (2,)), (0, (3,))) + tuple((b, es) for b in range(1, BLOCKS) for es in ((0, 1), (2, 3)))
-LAST_SUM_CUTS = (0, 384, T)
+RESULT_CUTS = ((0, 512, 768, 896, S),) + ((0, 512, S),) * (BLOCKS - 1)
+LAST_CUTS = (0, 384, T)
 
 FLOPS = 2 * S * (2 * K * H + H * N)
 
@@ -207,37 +207,43 @@ def tile_moe_pln_glu_silu_kernel(
                     stage(step - lag)
 
         y_sb = [keep.tile([P, S], F32, name=f"y_sb{b}") for b in range(BLOCKS)]
-        for index, (b, experts) in enumerate(RESULTS):
-            y_bank = bank([P, len(experts) * C])
-            for g, e in enumerate(experts):
-                nc.tensor.matmul_mx(
-                    out=y_bank[:, g * C : (g + 1) * C],
-                    lhsT=words[2][:, e, 2 * b * P : 2 * (b + 1) * P].bitcast(FP4X4),
-                    lhsT_scale=planes[2][:, e, b * P : (b + 1) * P],
-                    rhs=h_codes[e][:].bitcast(FP8X4),
-                    rhs_scale=h_scales[e][:],
-                    start=True,
-                    stop=True,
-                )
-            copy = nc.vector.tensor_copy if index == 0 else nc.scalar.copy
-            copy(y_sb[b][:, experts[0] * C : (experts[-1] + 1) * C], y_bank[:])
-
-        parts = {}
-
-        def pick(b, r):
-            parts[b, r] = work.tile([P, T], F32, name=f"part{r}")
-            nc.vector.tensor_tensor(parts[b, r][:], y_sb[b][:].indirect(pos_sb[r][:]), gates[r][:, b, :], MULT)
-
-        def add_and_store(b):
-            total = work.tile([P, T], F32, name="total")
-            cuts = LAST_SUM_CUTS if b == BLOCKS - 1 else (0, T)
-            for t0, t1 in zip(cuts[:-1], cuts[1:]):
-                nc.vector.tensor_tensor(total[:, t0:t1], parts[b, 0][:, t0:t1], parts[b, 1][:, t0:t1], ADD)
-                nc.sync.dma_start(out[b * P : (b + 1) * P, t0:t1], total[:, t0:t1])
-
         for b in range(BLOCKS):
-            pick(b, 0)
+            for s0, s1 in zip(RESULT_CUTS[b][:-1], RESULT_CUTS[b][1:]):
+                y_bank = bank([P, s1 - s0])
+                for e in range(s0 // C, (s1 + C - 1) // C):
+                    m0, m1 = max(s0, e * C), min(s1, (e + 1) * C)
+                    nc.tensor.matmul_mx(
+                        out=y_bank[:, m0 - s0 : m1 - s0],
+                        lhsT=words[2][:, e, 2 * b * P : 2 * (b + 1) * P].bitcast(FP4X4),
+                        lhsT_scale=planes[2][:, e, b * P : (b + 1) * P],
+                        rhs=h_codes[e][:, m0 - e * C : m1 - e * C].bitcast(FP8X4),
+                        rhs_scale=h_scales[e][:, m0 - e * C : m1 - e * C],
+                        start=True,
+                        stop=True,
+                    )
+                copy = nc.vector.tensor_copy if b == 0 and s0 == 0 else nc.scalar.copy
+                copy(y_sb[b][:, s0:s1], y_bank[:])
+
+        parts = {(b, r): work.tile([P, T], F32, name=f"part{r}") for b in range(BLOCKS) for r in range(2)}
+
+        def pick(b, r, t0, t1):
+            listed = pos_sb[r][:, t0 // LIST_ROWS : t1 // LIST_ROWS]
+            nc.vector.tensor_tensor(
+                parts[b, r][:, t0:t1], y_sb[b][:].indirect(listed), gates[r][:, b, t0:t1], MULT
+            )
+
+        def add_and_store(b, t0, t1):
+            total = work.tile([P, t1 - t0], F32, name="total")
+            nc.vector.tensor_tensor(total[:], parts[b, 0][:, t0:t1], parts[b, 1][:, t0:t1], ADD)
+            nc.sync.dma_start(out[b * P : (b + 1) * P, t0:t1], total[:])
+
+        last = BLOCKS - 1
+        last_pieces = list(zip(LAST_CUTS[:-1], LAST_CUTS[1:]))
+        for b in range(BLOCKS):
+            pick(b, 0, 0, T)
             if b > 0:
-                add_and_store(b - 1)
-            pick(b, 1)
-        add_and_store(BLOCKS - 1)
+                add_and_store(b - 1, 0, T)
+            for t0, t1 in last_pieces if b == last else [(0, T)]:
+                pick(b, 1, t0, t1)
+        for t0, t1 in last_pieces:
+            add_and_store(last, t0, t1)

from contextlib import ExitStack

import concourse.mybir as mybir
from concourse.masks import make_identity

F32 = mybir.dt.float32
BF16 = mybir.dt.bfloat16
I32 = mybir.dt.int32
U32 = mybir.dt.uint32
U16 = mybir.dt.uint16
U8 = mybir.dt.uint8
FP8X4 = mybir.dt.float8_e4m3fn_x4
FP4X4 = mybir.dt.float4_e2m1fn_x4
ADD, MULT = mybir.AluOpType.add, mybir.AluOpType.mult
SILU = mybir.ActivationFunctionType.Silu

P = 128
K, T, E, C, H, N = 512, 512, 4, 256, 512, 512
S = E * C
PACK = 4
UNIT = 128
UNITS = S // UNIT
UNITS_PER_EXPERT = C // UNIT
BLOCKS = N // P
LIST_ROWS = 16
PSUM_BANKS = 8

HALF = T // 2
X_ON_SCALAR = 96
GATHER_CUTS = (0, 256, 640, 1024)
ON_GPSIMD = (0,)
TURNED_OUT_ON_VECTOR = (4,)
LAST = E - 1
RESULT_CUTS = ((0, 512, 768, 896, S),) + ((0, 512, S),) * (BLOCKS - 1)
LAST_CUTS = (0, 384, T)

FLOPS = 2 * S * (2 * K * H + H * N)


def tile_moe_pln_glu_silu_kernel(
    tc, xT, w1_words, w1_scales, w3_words, w3_scales, w2_words, w2_scales, gate, offs, pos1, pos2, out
):
    nc = tc.nc
    with ExitStack() as ctx:
        keep = ctx.enter_context(tc.tile_pool(name="keep", bufs=1))
        work = ctx.enter_context(tc.tile_pool(name="work", bufs=8))
        psum = ctx.enter_context(tc.psum_pool(name="psum", bufs=PSUM_BANKS))

        def bank(shape):
            return psum.tile(shape, F32, name="bank")

        words = [keep.tile([P, E, 2 * H], U8, name=f"words{m}", align_bytes=64) for m in range(3)]
        planes = [keep.tile([P, E, H], U8, name=f"planes{m}", align_bytes=64) for m in range(3)]

        def zero_planes(m):
            nc.vector.memset(planes[m][:].rearrange("p e i -> p (e i)").bitcast(I32), 0)

        def load_words(m, dram, e0, e1):
            nc.sync.dma_start(
                words[m][:, e0:e1, :].bitcast(I32), dram.bitcast(I32)[e0:e1].rearrange("e o p i -> p (e o) i")
            )

        def load_scales(engines, m, dram):
            rows = dram.bitcast(I32).rearrange("e o (Q r) i -> r Q (e o) i", r=4)
            for r, engine in enumerate(engines):
                engine.dma_start(planes[m][:].bitcast(I32)[r : P : 32], rows[r])

        x_raw = [keep.tile([P, PACK, HALF], F32, name=f"x_raw{h}", align_bytes=64) for h in range(2)]
        for h in range(2):
            nc.sync.dma_start(x_raw[h][:], xT.rearrange("(p j) t -> p j t", j=PACK)[:, :, h * HALF : (h + 1) * HALF])
        offs_sb = keep.tile([P, S // LIST_ROWS], U16, name="offs_sb")
        nc.sync.dma_start(offs_sb[:], offs)

        x_scales = keep.tile([P, T], U8, name="x_scales", align_bytes=64)
        nc.gpsimd.memset(x_scales[:], 0)
        warm = keep.tile([P, 1], F32, name="warm")
        nc.vector.memset(warm[:], 0.0)
        zero_planes(0)
        zero_planes(1)
        load_words(0, w1_words, 0, 1)
        load_words(1, w3_words, 0, 1)
        load_scales([nc.scalar, nc.scalar, nc.scalar, nc.sync], 0, w1_scales)
        load_scales([nc.sync] * 4, 1, w3_scales)
        nc.scalar.activation(warm[:], warm[:], SILU)
        zero_planes(2)
        ident = keep.tile([P, P], F32, name="ident")
        make_identity(nc, ident[:])
        load_words(0, w1_words, 1, E)
        load_words(1, w3_words, 1, E)
        load_scales([nc.sync] * 4, 2, w2_scales)
        load_words(2, w2_words, 0, E)
        pos_sb = [keep.tile([P, T // LIST_ROWS], U16, name=f"pos_sb{r}") for r in range(2)]
        nc.sync.dma_start(pos_sb[0][:], pos1)
        nc.sync.dma_start(pos_sb[1][:], pos2)
        gates = [keep.tile([P, BLOCKS, T], F32, name=f"gates{r}") for r in range(2)]
        for r in range(2):
            nc.sync.dma_start(gates[r][:], gate[r].rearrange("(b p) t -> p b t", p=P))

        x_codes = keep.tile([P, T], U32, name="x_codes", align_bytes=64)
        for h in range(2):
            x_bf = keep.tile([P, HALF, PACK], BF16, name=f"x_bf{h}", align_bytes=64)
            source = x_raw[h][:].rearrange("p j t -> p t j")
            nc.scalar.copy(x_bf[:, :X_ON_SCALAR, :], source[:, :X_ON_SCALAR, :])
            nc.vector.tensor_copy(x_bf[:, X_ON_SCALAR:, :], source[:, X_ON_SCALAR:, :])
            tokens = slice(h * HALF, (h + 1) * HALF)
            nc.vector.quantize_mx(
                out=x_codes[:, tokens].bitcast(FP8X4),
                scales=x_scales[:, tokens],
                in_=x_bf[:].rearrange("p t j -> p (t j)"),
            )

        slot_codes, slot_scales = {}, {}
        for cut, (s0, s1) in enumerate(zip(GATHER_CUTS[:-1], GATHER_CUTS[1:])):
            listed = offs_sb[:, s0 // LIST_ROWS : s1 // LIST_ROWS]
            scales = keep.tile([P, s1 - s0], U8, name=f"slot_scales{cut}", align_bytes=64)
            codes = keep.tile([P, s1 - s0], U32, name=f"slot_codes{cut}", align_bytes=64)
            nc.vector.tensor_copy(scales[:], x_scales[:].indirect(listed))
            nc.vector.tensor_copy(codes[:], x_codes[:].indirect(listed))
            for s in range(s0, s1, UNIT):
                slot_codes[s // UNIT] = codes[:, s - s0 : s - s0 + UNIT]
                slot_scales[s // UNIT] = scales[:, s - s0 : s - s0 + UNIT]

        h_codes = [keep.tile([P, C], U32, name=f"h_codes{e}", align_bytes=64) for e in range(E)]
        h_scales = [keep.tile([P, C], U8, name=f"h_scales{e}", align_bytes=64) for e in range(E)]
        a_banks, b_banks, act, up, hidden, turned, hidden_k = {}, {}, {}, {}, {}, {}, {}

        def first_product(banks, m, unit):
            e = unit // UNITS_PER_EXPERT
            banks[unit] = bank([P, H])
            nc.tensor.matmul_mx(
                out=banks[unit][:],
                lhsT=slot_codes[unit].bitcast(FP8X4),
                lhsT_scale=slot_scales[unit],
                rhs=words[m][:, e, :].bitcast(FP4X4),
                rhs_scale=planes[m][:, e, :],
                start=True,
                stop=True,
            )

        def gate_product(unit):
            first_product(a_banks, 0, unit)

        def up_product(unit):
            first_product(b_banks, 1, unit)

        def activate(unit):
            act[unit] = work.tile([P, H], F32, name="act")
            nc.scalar.activation(act[unit][:], a_banks[unit][:], SILU)

        def copy_up(unit):
            if unit in ON_GPSIMD:
                up[unit] = work.tile([P, H], F32, name="up")
                nc.scalar.copy(up[unit][:], b_banks[unit][:])

        def multiply(unit):
            hidden[unit] = work.tile([P, H], BF16, name="hidden")
            if unit in ON_GPSIMD:
                nc.gpsimd.tensor_tensor(hidden[unit][:], act[unit][:], up[unit][:], MULT)
            else:
                nc.vector.tensor_tensor(hidden[unit][:], act[unit][:], b_banks[unit][:], MULT)

        def turn(unit):
            pairs = hidden[unit][:].bitcast(F32)
            turned[unit] = bank([P, 2, UNIT])
            for u in range(2):
                nc.tensor.transpose(turned[unit][:, u, :], pairs[:, u : H // 2 : 2], ident[:])

        def turn_out(unit):
            e, place = unit // UNITS_PER_EXPERT, unit % UNITS_PER_EXPERT
            if e == LAST or place == 0:
                joined = 1 if e == LAST else UNITS_PER_EXPERT
                hidden_k[unit] = work.tile([P, joined * UNIT * PACK], BF16, name="hidden_k", align_bytes=64)
            else:
                hidden_k[unit] = hidden_k[unit - place]
            s0 = 0 if e == LAST else place * UNIT
            copy = nc.vector.tensor_copy if unit in TURNED_OUT_ON_VECTOR else nc.scalar.copy
            copy(
                hidden_k[unit][:, s0 * PACK : (s0 + UNIT) * PACK].bitcast(F32).rearrange("p (s u) -> p s u", u=2),
                turned[unit][:].rearrange("p u s -> p s u"),
            )

        def quantise(unit):
            e, place = unit // UNITS_PER_EXPERT, unit % UNITS_PER_EXPERT
            if e == LAST:
                slots = slice(place * UNIT, (place + 1) * UNIT)
            elif place == UNITS_PER_EXPERT - 1:
                slots = slice(0, C)
            else:
                return
            nc.vector.quantize_mx(
                out=h_codes[e][:, slots].bitcast(FP8X4), scales=h_scales[e][:, slots], in_=hidden_k[unit][:]
            )

        stages = (
            (gate_product, 0),
            (up_product, 1),
            (activate, 0),
            (copy_up, 1),
            (multiply, 1),
            (turn, UNITS - 1),
            (turn_out, UNITS - 1),
            (quantise, UNITS),
        )
        for step in range(2 * UNITS):
            for stage, lag in stages:
                if 0 <= step - lag < UNITS:
                    stage(step - lag)

        y_sb = [keep.tile([P, S], F32, name=f"y_sb{b}") for b in range(BLOCKS)]
        for b in range(BLOCKS):
            for s0, s1 in zip(RESULT_CUTS[b][:-1], RESULT_CUTS[b][1:]):
                y_bank = bank([P, s1 - s0])
                for e in range(s0 // C, (s1 + C - 1) // C):
                    m0, m1 = max(s0, e * C), min(s1, (e + 1) * C)
                    nc.tensor.matmul_mx(
                        out=y_bank[:, m0 - s0 : m1 - s0],
                        lhsT=words[2][:, e, 2 * b * P : 2 * (b + 1) * P].bitcast(FP4X4),
                        lhsT_scale=planes[2][:, e, b * P : (b + 1) * P],
                        rhs=h_codes[e][:, m0 - e * C : m1 - e * C].bitcast(FP8X4),
                        rhs_scale=h_scales[e][:, m0 - e * C : m1 - e * C],
                        start=True,
                        stop=True,
                    )
                copy = nc.vector.tensor_copy if b == 0 and s0 == 0 else nc.scalar.copy
                copy(y_sb[b][:, s0:s1], y_bank[:])

        parts = {(b, r): work.tile([P, T], F32, name=f"part{r}") for b in range(BLOCKS) for r in range(2)}

        def pick(b, r, t0, t1):
            listed = pos_sb[r][:, t0 // LIST_ROWS : t1 // LIST_ROWS]
            nc.vector.tensor_tensor(
                parts[b, r][:, t0:t1], y_sb[b][:].indirect(listed), gates[r][:, b, t0:t1], MULT
            )

        def add_and_store(b, t0, t1):
            total = work.tile([P, t1 - t0], F32, name="total")
            nc.vector.tensor_tensor(total[:], parts[b, 0][:, t0:t1], parts[b, 1][:, t0:t1], ADD)
            nc.sync.dma_start(out[b * P : (b + 1) * P, t0:t1], total[:])

        last = BLOCKS - 1
        last_pieces = list(zip(LAST_CUTS[:-1], LAST_CUTS[1:]))
        for b in range(BLOCKS):
            pick(b, 0, 0, T)
            if b > 0:
                add_and_store(b - 1, 0, T)
            for t0, t1 in last_pieces if b == last else [(0, T)]:
                pick(b, 1, t0, t1)
        for t0, t1 in last_pieces:
            add_and_store(last, t0, t1)
